import numpy as np
import ml_dtypes


def mxq(x, axis, fmt="e4m3"):
    dtype, down = {"e4m3": (ml_dtypes.float8_e4m3fn, 7), "e5m2": (ml_dtypes.float8_e5m2, 14)}[fmt]
    v = np.moveaxis(np.asarray(x, np.float32).astype(ml_dtypes.bfloat16).astype(np.float64), axis, -1)
    blocks = v.reshape(v.shape[:-1] + (-1, 32))
    amax = np.abs(blocks).max(-1, keepdims=True)
    byte = np.maximum(np.where(amax > 0, np.frexp(amax)[1] - 1 + 127, 0) - down, 1)
    scale = np.exp2(byte - 127.0)
    codes = (blocks / scale).astype(np.float32).astype(dtype).astype(np.float64)
    return np.moveaxis((codes * scale).reshape(v.shape), -1, axis)


WIDE = False


def mx_kscale(k):
    if not WIDE:
        return np.ones(k)
    levels = np.array([10, -10, 5, -5, 0])
    if k % 512:
        return np.exp2(np.random.permutation(np.resize(levels, k // 32))).repeat(32)
    a = np.empty((k // 512, 16))
    for p in range(k // 512):
        a[p, :8] = np.random.permutation(np.resize(levels, 8))
        for g in range(8):
            far = levels[np.abs(levels - a[p, g]) >= 10]
            a[p, g + 8] = far[np.random.randint(len(far))]
    return np.exp2(a.ravel()).repeat(32)


def f64(x):
    return np.asarray(x).astype(np.float64)


def striped(idx):
    return np.tile(idx.reshape(-1, 16).T, (8, 1)).astype(np.uint16)


def unstriped(offs):
    return offs[:16].T.reshape(-1).astype(np.int64)


E2M1 = np.array([0.0, 0.5, 1.0, 1.5, 2.0, 3.0, 4.0, 6.0, -0.0, -0.5, -1.0, -1.5, -2.0, -3.0, -4.0, -6.0])


def pack_weight(w, fmt):
    k, n = w.shape
    w = f64(np.asarray(w, np.float32).astype(ml_dtypes.bfloat16)).reshape(k // 32, 32, n)
    amax = np.abs(w).max(1)
    if fmt == "e4m3":
        byte = np.frexp(amax)[1] - 1 + 127 - 7
    else:
        mant, ex = np.frexp(amax / 6.0)
        byte = np.where(mant > 0.5, ex, ex - 1) + 127
    byte = np.clip(np.where(amax > 0, byte, 1), 1, 254)
    scaled = (w * np.exp2(127.0 - byte)[:, None, :]).reshape(k, n).astype(np.float32)
    by_word = np.ascontiguousarray(scaled.reshape(k // 512, 128, 4, n).transpose(0, 1, 3, 2))
    if fmt == "e4m3":
        words = by_word.astype(ml_dtypes.float8_e4m3fn).view(np.uint8)
    else:
        c = by_word.astype(ml_dtypes.float4_e2m1fn).view(np.uint8) & 0xF
        words = (c[..., 0::2] | (c[..., 1::2] << 4)).reshape(k // 512, 128, 2 * n)
    return np.ascontiguousarray(words), np.ascontiguousarray(byte.astype(np.uint8).reshape(k // 512, 16, n))


def unpack_weight(words, scales, fmt):
    g, _, n = scales.shape
    words = np.ascontiguousarray(words).reshape(g, 128, n, -1)
    if fmt == "e4m3":
        vals = words.view(ml_dtypes.float8_e4m3fn).astype(np.float64)
    else:
        nib = np.empty((g, 128, n, 4), np.uint8)
        nib[..., 0::2] = words & 0xF
        nib[..., 1::2] = words >> 4
        vals = E2M1[nib]
    vals = vals * np.repeat(np.exp2(scales.astype(np.float64) - 127.0), 8, axis=1)[..., None]
    return vals.transpose(0, 1, 3, 2).reshape(g * 512, n)


G, K, M, T, S = 4, 512, 512, 2048, 256


def setup_inputs():
    n = np.random.standard_normal
    s = mx_kscale(K)[:, None]
    p_w4 = pack_weight(n((K, M)) / np.sqrt(K) / s, "e2m1")
    p_w8 = pack_weight(n((K, M)) / np.sqrt(K) / s, "e4m3")
    return {
        "xT": (n((K, T)) * s).astype(np.float32),
        "c": (n((K, S)) * s).astype(np.float32),
        "w4_words": p_w4[0],
        "w4_scales": p_w4[1],
        "w8_words": p_w8[0],
        "w8_scales": p_w8[1],
        "r": (n((256, 512))).astype(np.float32),
        "offs": striped(np.concatenate([np.random.permutation(T)[:S] for _ in range(G)])),
    }


def reference(xT, c, w4_words, w4_scales, w8_words, w8_scales, r, offs):
    idx = unstriped(offs).reshape(G, S)
    xm_ = mxq(np.max([f64(xT)[:, idx[g]] for g in range(G)], axis=0), 0, "e4m3")
    c_ = mxq(f64(c), 0, "e4m3")
    w4_ = unpack_weight(w4_words, w4_scales, "e2m1")
    w8_ = unpack_weight(w8_words, w8_scales, "e4m3")
    y = xm_.T @ w4_ + c_.T @ w8_
    return f64(r) + y

@@ -1,0 +1,122 @@
+from contextlib import ExitStack
+
+import concourse.mybir as mybir
+
+G, K, M, T, S = 4, 512, 512, 2048, 256
+FLOPS = 2 * 2 * K * M * S
+
+F32 = mybir.dt.float32
+BF16 = mybir.dt.bfloat16
+I32 = mybir.dt.int32
+U32 = mybir.dt.uint32
+U16 = mybir.dt.uint16
+U8 = mybir.dt.uint8
+FP8X4 = mybir.dt.float8_e4m3fn_x4
+FP4X4 = mybir.dt.float4_e2m1fn_x4
+MAX = mybir.AluOpType.max
+ADD = mybir.AluOpType.add
+
+P = 128
+HALVES = S // P
+CHUNKS = (((1024, 1024), (1024, 704)), ((512, 0), (512, 0), (512, 0), (512, 352)))
+
+
+def tile_list_sage_tm_res_kernel(tc, xT, c, w4_words, w4_scales, w8_words, w8_scales, r, offs, out):
+    nc = tc.nc
+    with ExitStack() as ctx:
+        keep = ctx.enter_context(tc.tile_pool(name="keep", bufs=1))
+        psum = ctx.enter_context(tc.psum_pool(name="psum", bufs=1))
+
+        offsets = keep.tile([P, G * S // 16], U16, name="offsets")
+        w_scales = keep.tile([P, 2 * M], U8, name="w_scales", align_bytes=64)
+
+        x_rows = xT.rearrange("(p i) t -> p i t", i=4)
+        raw = {}
+        for pair in range(2):
+            start = 0
+            for n, (width, on_vector) in enumerate(CHUNKS[pair]):
+                raw[pair, n] = keep.tile([P, 2, width], F32, name="raw_%d_%d" % (pair, n))
+                nc.sync.dma_start(raw[pair, n][:], x_rows[:, 2 * pair : 2 * pair + 2, start : start + width])
+                start = start + width
+                if pair == 0 and n == 0:
+                    nc.sync.dma_start(offsets[:], offs)
+                    for which, scales in enumerate((w8_scales, w4_scales)):
+                        for q in range(4):
+                            nc.scalar.dma_start(
+                                w_scales[32 * q : 32 * q + 4, which * M : (which + 1) * M].bitcast(I32),
+                                scales[0, 4 * q : 4 * q + 4, :].bitcast(I32),
+                            )
+
+        c_raw = keep.tile([P, 4, S], F32, name="c_raw")
+        nc.sync.dma_start(c_raw[:], c.rearrange("(p i) j -> p i j", i=4))
+        w8 = keep.tile([P, M], U32, name="w8", align_bytes=64)
+        nc.sync.dma_start(w8[:].bitcast(I32), w8_words[0].rearrange("p n t -> p (n t)").bitcast(I32))
+        w4 = keep.tile([P, 2 * M], U8, name="w4", align_bytes=64)
+        nc.sync.dma_start(w4[:].bitcast(I32), w4_words[0].bitcast(I32))
+        r_sb = keep.tile([P, HALVES, M], F32, name="r_sb")
+        nc.sync.dma_start(r_sb[:], r.rearrange("(h p) n -> p h n", p=P))
+
+        part = [keep.tile([P, 2, 4 * P], BF16, name="part_%d" % h, align_bytes=64) for h in range(HALVES)]
+        c_codes = [keep.tile([P, P], U32, name="c_codes_%d" % h, align_bytes=64) for h in range(HALVES)]
+        c_scales = [keep.tile([P, P], U8, name="c_scales_%d" % h, align_bytes=64) for h in range(HALVES)]
+        for pair in range(2):
+            table = keep.tile([P, 2 * T], BF16, name="table_%d" % pair)
+            start = 0
+            for n, (width, on_vector) in enumerate(CHUNKS[pair]):
+                src = raw[pair, n][:].rearrange("p e t -> p t e")
+                dst = table[:, 2 * start : 2 * (start + width)].rearrange("p (t e) -> p t e", e=2)
+                if on_vector > 0:
+                    nc.vector.tensor_copy(dst[:, :on_vector, :], src[:, :on_vector, :])
+                if on_vector < width:
+                    nc.scalar.copy(dst[:, on_vector:, :], src[:, on_vector:, :])
+                start = start + width
+            picked = keep.tile([P, G * S], U32, name="picked_%d" % pair)
+            nc.vector.tensor_copy(picked[:], table[:].bitcast(U32).indirect(offsets[:]))
+            if pair == 1:
+                for h in range(HALVES):
+                    nc.scalar.copy(
+                        part[h][:, 1, :].rearrange("p (a b i) -> p a i b", b=4, i=4),
+                        c_raw[:, :, h * P : (h + 1) * P].rearrange("p i (a b) -> p a i b", b=4),
+                    )
+                    nc.vector.quantize_mx(out=c_codes[h][:].bitcast(FP8X4), scales=c_scales[h][:], in_=part[h][:, 1, :])
+            values = picked[:].bitcast(BF16).rearrange("p (g h w) -> p g h w", g=G, h=HALVES)
+            for h in range(HALVES):
+                nc.vector.tensor_tensor(
+                    part[h][:, pair, :].rearrange("p (u w) -> p u w", u=2), values[:, 0:2, h, :], values[:, 2:4, h, :], MAX
+                )
+
+        x_grouped = [keep.tile([P, 4 * P], BF16, name="x_grouped_%d" % h, align_bytes=64) for h in range(HALVES)]
+        for h in range(HALVES):
+            both = part[h][:].rearrange("p q (u j e) -> p u j q e", u=2, e=2)
+            nc.vector.tensor_tensor(
+                x_grouped[h][:].rearrange("p (j q e) -> p j q e", q=2, e=2), both[:, 0], both[:, 1], MAX
+            )
+        x_codes = [keep.tile([P, P], U32, name="x_codes_%d" % h, align_bytes=64) for h in range(HALVES)]
+        x_scales = [keep.tile([P, P], U8, name="x_scales_%d" % h, align_bytes=64) for h in range(HALVES)]
+        for h in range(HALVES):
+            nc.vector.quantize_mx(out=x_codes[h][:].bitcast(FP8X4), scales=x_scales[h][:], in_=x_grouped[h][:])
+
+        acc = [psum.tile([P, M], F32, name="acc_%d" % h) for h in range(HALVES)]
+        for h in range(HALVES):
+            nc.tensor.matmul_mx(
+                out=acc[h][:],
+                lhsT=c_codes[h][:].bitcast(FP8X4),
+                lhsT_scale=c_scales[h][:],
+                rhs=w8[:].bitcast(FP8X4),
+                rhs_scale=w_scales[:, 0:M],
+                start=True,
+                stop=False,
+            )
+            nc.tensor.matmul_mx(
+                out=acc[h][:],
+                lhsT=x_codes[h][:].bitcast(FP8X4),
+                lhsT_scale=x_scales[h][:],
+                rhs=w4[:].bitcast(FP4X4),
+                rhs_scale=w_scales[:, M : 2 * M],
+                start=False,
+                stop=True,
+            )
+        for h in range(HALVES):
+            result = keep.tile([P, M], F32, name="result_%d" % h)
+            nc.vector.tensor_tensor(result[:], acc[h][:], r_sb[:, h, :], ADD)
+            nc.sync.dma_start(out[h * P : (h + 1) * P, :], result[:])

@@ -19,6 +19,7 @@ ADD = mybir.AluOpType.add
 P = 128
 HALVES = S // P
 CHUNKS = (((1024, 1024), (1024, 704)), ((512, 0), (512, 0), (512, 0), (512, 352)))
+BANKS = ((0, 256), (256, 256))
 
 
 def tile_list_sage_tm_res_kernel(tc, xT, c, w4_words, w4_scales, w8_words, w8_scales, r, offs, out):
@@ -38,25 +39,27 @@ def tile_list_sage_tm_res_kernel(tc, xT, c, w4_words, w4_scales, w8_words, w8_sc
                 raw[pair, n] = keep.tile([P, 2, width], F32, name="raw_%d_%d" % (pair, n))
                 nc.sync.dma_start(raw[pair, n][:], x_rows[:, 2 * pair : 2 * pair + 2, start : start + width])
                 start = start + width
-                if pair == 0 and n == 0:
+                if pair == 0 and n == len(CHUNKS[0]) - 1:
                     nc.sync.dma_start(offsets[:], offs)
-                    for which, scales in enumerate((w8_scales, w4_scales)):
-                        for q in range(4):
-                            nc.scalar.dma_start(
-                                w_scales[32 * q : 32 * q + 4, which * M : (which + 1) * M].bitcast(I32),
-                                scales[0, 4 * q : 4 * q + 4, :].bitcast(I32),
-                            )
 
-        c_raw = keep.tile([P, 4, S], F32, name="c_raw")
-        nc.sync.dma_start(c_raw[:], c.rearrange("(p i) j -> p i j", i=4))
+        stage = keep.tile([P, 2 * S + 4 * S], F32, name="stage")
+        c_raw = stage[:, 2 * S :].rearrange("p (i j) -> p i j", i=4)
+        part = stage[:, : 4 * S].bitcast(BF16).rearrange("p (q h u w) -> p q h u w", q=2, h=HALVES, u=2)
+        nc.sync.dma_start(c_raw, c.rearrange("(p i) j -> p i j", i=4))
         w8 = keep.tile([P, M], U32, name="w8", align_bytes=64)
         nc.sync.dma_start(w8[:].bitcast(I32), w8_words[0].rearrange("p n t -> p (n t)").bitcast(I32))
         w4 = keep.tile([P, 2 * M], U8, name="w4", align_bytes=64)
         nc.sync.dma_start(w4[:].bitcast(I32), w4_words[0].bitcast(I32))
+        for which, scales in enumerate((w8_scales, w4_scales)):
+            for q in range(4):
+                nc.sync.dma_start(
+                    w_scales[32 * q : 32 * q + 4, which * M : (which + 1) * M].bitcast(I32),
+                    scales[0, 4 * q : 4 * q + 4, :].bitcast(I32),
+                )
         r_sb = keep.tile([P, HALVES, M], F32, name="r_sb")
         nc.sync.dma_start(r_sb[:], r.rearrange("(h p) n -> p h n", p=P))
 
-        part = [keep.tile([P, 2, 4 * P], BF16, name="part_%d" % h, align_bytes=64) for h in range(HALVES)]
+        c_grouped = [keep.tile([P, 4 * P], BF16, name="c_grouped_%d" % h, align_bytes=64) for h in range(HALVES)]
         c_codes = [keep.tile([P, P], U32, name="c_codes_%d" % h, align_bytes=64) for h in range(HALVES)]
         c_scales = [keep.tile([P, P], U8, name="c_scales_%d" % h, align_bytes=64) for h in range(HALVES)]
         for pair in range(2):
@@ -72,51 +75,68 @@ def tile_list_sage_tm_res_kernel(tc, xT, c, w4_words, w4_scales, w8_words, w8_sc
                 start = start + width
             picked = keep.tile([P, G * S], U32, name="picked_%d" % pair)
             nc.vector.tensor_copy(picked[:], table[:].bitcast(U32).indirect(offsets[:]))
+            values = picked[:].bitcast(BF16).rearrange("p (g h w) -> p g h w", g=G, h=HALVES)
             if pair == 1:
                 for h in range(HALVES):
                     nc.scalar.copy(
-                        part[h][:, 1, :].rearrange("p (a b i) -> p a i b", b=4, i=4),
+                        c_grouped[h][:].rearrange("p (a b i) -> p a i b", b=4, i=4),
                         c_raw[:, :, h * P : (h + 1) * P].rearrange("p i (a b) -> p a i b", b=4),
                     )
-                    nc.vector.quantize_mx(out=c_codes[h][:].bitcast(FP8X4), scales=c_scales[h][:], in_=part[h][:, 1, :])
-            values = picked[:].bitcast(BF16).rearrange("p (g h w) -> p g h w", g=G, h=HALVES)
-            for h in range(HALVES):
-                nc.vector.tensor_tensor(
-                    part[h][:, pair, :].rearrange("p (u w) -> p u w", u=2), values[:, 0:2, h, :], values[:, 2:4, h, :], MAX
-                )
+            if pair == 0:
+                for h in range(HALVES):
+                    nc.vector.tensor_tensor(part[:, pair, h], values[:, 0:2, h, :], values[:, 2:4, h, :], MAX)
 
         x_grouped = [keep.tile([P, 4 * P], BF16, name="x_grouped_%d" % h, align_bytes=64) for h in range(HALVES)]
-        for h in range(HALVES):
-            both = part[h][:].rearrange("p q (u j e) -> p u j q e", u=2, e=2)
+        x_codes = [keep.tile([P, P], U32, name="x_codes_%d" % h, align_bytes=64) for h in range(HALVES)]
+        x_scales = [keep.tile([P, P], U8, name="x_scales_%d" % h, align_bytes=64) for h in range(HALVES)]
+
+        def qc(h):
+            nc.vector.quantize_mx(out=c_codes[h][:].bitcast(FP8X4), scales=c_scales[h][:], in_=c_grouped[h][:])
+
+        def l1(h):
+            nc.vector.tensor_tensor(part[:, 1, h], values[:, 0:2, h, :], values[:, 2:4, h, :], MAX)
+
+        def l2(h):
+            both = part[:, :, h].rearrange("p q u (j e) -> p u j q e", e=2)
             nc.vector.tensor_tensor(
                 x_grouped[h][:].rearrange("p (j q e) -> p j q e", q=2, e=2), both[:, 0], both[:, 1], MAX
             )
-        x_codes = [keep.tile([P, P], U32, name="x_codes_%d" % h, align_bytes=64) for h in range(HALVES)]
-        x_scales = [keep.tile([P, P], U8, name="x_scales_%d" % h, align_bytes=64) for h in range(HALVES)]
-        for h in range(HALVES):
+
+        def qx(h):
             nc.vector.quantize_mx(out=x_codes[h][:].bitcast(FP8X4), scales=x_scales[h][:], in_=x_grouped[h][:])
 
-        acc = [psum.tile([P, M], F32, name="acc_%d" % h) for h in range(HALVES)]
+        qc(0)
+        l1(0)
+        qc(1)
+        l1(1)
+        l2(0)
+        l2(1)
+        qx(0)
+        qx(1)
+
         for h in range(HALVES):
-            nc.tensor.matmul_mx(
-                out=acc[h][:],
-                lhsT=c_codes[h][:].bitcast(FP8X4),
-                lhsT_scale=c_scales[h][:],
-                rhs=w8[:].bitcast(FP8X4),
-                rhs_scale=w_scales[:, 0:M],
-                start=True,
-                stop=False,
-            )
-            nc.tensor.matmul_mx(
-                out=acc[h][:],
-                lhsT=x_codes[h][:].bitcast(FP8X4),
-                lhsT_scale=x_scales[h][:],
-                rhs=w4[:].bitcast(FP4X4),
-                rhs_scale=w_scales[:, M : 2 * M],
-                start=False,
-                stop=True,
-            )
-        for h in range(HALVES):
-            result = keep.tile([P, M], F32, name="result_%d" % h)
-            nc.vector.tensor_tensor(result[:], acc[h][:], r_sb[:, h, :], ADD)
-            nc.sync.dma_start(out[h * P : (h + 1) * P, :], result[:])
+            for start, width in BANKS:
+                acc = psum.tile([P, width], F32, name="acc_%d_%d" % (h, start))
+                nc.tensor.matmul_mx(
+                    out=acc[:],
+                    lhsT=c_codes[h][:].bitcast(FP8X4),
+                    lhsT_scale=c_scales[h][:],
+                    rhs=w8[:, start : start + width].bitcast(FP8X4),
+                    rhs_scale=w_scales[:, start : start + width],
+                    start=True,
+                    stop=False,
+                )
+                step = M if width == M else P
+                for n in range(0, width, step):
+                    nc.tensor.matmul_mx(
+                        out=acc[:, n : n + step],
+                        lhsT=x_codes[h][:].bitcast(FP8X4),
+                        lhsT_scale=x_scales[h][:],
+                        rhs=w4[:, 2 * (start + n) : 2 * (start + n + step)].bitcast(FP4X4),
+                        rhs_scale=w_scales[:, M + start + n : M + start + n + step],
+                        start=False,
+                        stop=(n + step == width),
+                    )
+                result = keep.tile([P, width], F32, name="result_%d_%d" % (h, start))
+                nc.vector.tensor_tensor(result[:], acc[:], r_sb[:, h, start : start + width], ADD)
+                nc.sync.dma_start(out[h * P : (h + 1) * P, start : start + width], result[:])

@@ -18,8 +18,13 @@ ADD = mybir.AluOpType.add
 
 P = 128
 HALVES = S // P
-CHUNKS = (((1024, 1024), (1024, 704)), ((512, 0), (512, 0), (512, 0), (512, 352)))
-BANKS = ((0, 256), (256, 256))
+CHUNKS = ((768, 0), (768, 256), (512, 352))
+BANKS = (((0, 256), (256, 256)), ((0, 256), (256, 256)))
+
+
+def load_scale_rows(nc, plane, scales):
+    for q in range(4):
+        nc.sync.dma_start(plane[32 * q : 32 * q + 4, :].bitcast(I32), scales[0, 4 * q : 4 * q + 4, :].bitcast(I32))
 
 
 def tile_list_sage_tm_res_kernel(tc, xT, c, w4_words, w4_scales, w8_words, w8_scales, r, offs, out):
@@ -29,113 +34,102 @@ def tile_list_sage_tm_res_kernel(tc, xT, c, w4_words, w4_scales, w8_words, w8_sc
         psum = ctx.enter_context(tc.psum_pool(name="psum", bufs=1))
 
         offsets = keep.tile([P, G * S // 16], U16, name="offsets")
-        w_scales = keep.tile([P, 2 * M], U8, name="w_scales", align_bytes=64)
-
         x_rows = xT.rearrange("(p i) t -> p i t", i=4)
-        raw = {}
-        for pair in range(2):
-            start = 0
-            for n, (width, on_vector) in enumerate(CHUNKS[pair]):
-                raw[pair, n] = keep.tile([P, 2, width], F32, name="raw_%d_%d" % (pair, n))
-                nc.sync.dma_start(raw[pair, n][:], x_rows[:, 2 * pair : 2 * pair + 2, start : start + width])
-                start = start + width
-                if pair == 0 and n == len(CHUNKS[0]) - 1:
-                    nc.sync.dma_start(offsets[:], offs)
+        plane = [keep.tile([P, T], F32, name="plane_%d" % i) for i in range(2)]
+        nc.sync.dma_start(plane[0][:], x_rows[:, 0, :])
+        nc.sync.dma_start(offsets[:], offs)
+        nc.sync.dma_start(plane[1][:], x_rows[:, 1, :])
+        raw = []
+        start = 0
+        for n, (width, on_vector) in enumerate(CHUNKS):
+            raw.append(keep.tile([P, 2, width], F32, name="raw_%d" % n))
+            nc.sync.dma_start(raw[n][:], x_rows[:, 2:4, start : start + width])
+            start = start + width
 
-        stage = keep.tile([P, 2 * S + 4 * S], F32, name="stage")
-        c_raw = stage[:, 2 * S :].rearrange("p (i j) -> p i j", i=4)
-        part = stage[:, : 4 * S].bitcast(BF16).rearrange("p (q h u w) -> p q h u w", q=2, h=HALVES, u=2)
+        stage = keep.tile([P, S + 4 * S], F32, name="stage")
+        c_raw = stage[:, S:].rearrange("p (i j) -> p i j", i=4)
+        rows = stage[:, : 3 * S].bitcast(BF16).rearrange("p (n w) -> p n w", w=2 * P)
         nc.sync.dma_start(c_raw, c.rearrange("(p i) j -> p i j", i=4))
         w8 = keep.tile([P, M], U32, name="w8", align_bytes=64)
         nc.sync.dma_start(w8[:].bitcast(I32), w8_words[0].rearrange("p n t -> p (n t)").bitcast(I32))
         w4 = keep.tile([P, 2 * M], U8, name="w4", align_bytes=64)
         nc.sync.dma_start(w4[:].bitcast(I32), w4_words[0].bitcast(I32))
-        for which, scales in enumerate((w8_scales, w4_scales)):
-            for q in range(4):
-                nc.sync.dma_start(
-                    w_scales[32 * q : 32 * q + 4, which * M : (which + 1) * M].bitcast(I32),
-                    scales[0, 4 * q : 4 * q + 4, :].bitcast(I32),
-                )
+        w8_plane = keep.tile([P, M], U8, name="w8_plane", align_bytes=64)
+        load_scale_rows(nc, w8_plane, w8_scales)
         r_sb = keep.tile([P, HALVES, M], F32, name="r_sb")
         nc.sync.dma_start(r_sb[:], r.rearrange("(h p) n -> p h n", p=P))
+        w4_plane = keep.tile([P, M], U8, name="w4_plane", align_bytes=64)
+        load_scale_rows(nc, w4_plane, w4_scales)
 
-        c_grouped = [keep.tile([P, 4 * P], BF16, name="c_grouped_%d" % h, align_bytes=64) for h in range(HALVES)]
+        picked_low = keep.tile([P, 2, G * S], BF16, name="picked_low")
+        for i in range(2):
+            nc.vector.tensor_copy(picked_low[:, i, :], plane[i][:].indirect(offsets[:]))
+        low = keep.tile([P, 2, 2 * S], BF16, name="low")
+        nc.vector.tensor_tensor(low[:], picked_low[:, :, : 2 * S], picked_low[:, :, 2 * S :], MAX)
+        low_u = low[:].rearrange("p e (u h j) -> p u h j e", u=2, h=HALVES)
+        for h in range(HALVES):
+            nc.vector.tensor_tensor(rows[:, h, :].rearrange("p (j e) -> p j e", e=2), low_u[:, 0, h], low_u[:, 1, h], MAX)
+
+        table = keep.tile([P, 2 * T], BF16, name="table")
+        start = 0
+        for n, (width, on_vector) in enumerate(CHUNKS):
+            src = raw[n][:].rearrange("p e t -> p t e")
+            dst = table[:, 2 * start : 2 * (start + width)].rearrange("p (t e) -> p t e", e=2)
+            if on_vector > 0:
+                nc.vector.tensor_copy(dst[:, :on_vector, :], src[:, :on_vector, :])
+            if on_vector < width:
+                nc.scalar.copy(dst[:, on_vector:, :], src[:, on_vector:, :])
+            start = start + width
+        picked_high = keep.tile([P, G * S], U32, name="picked_high")
+        nc.vector.tensor_copy(picked_high[:], table[:].bitcast(U32).indirect(offsets[:]))
+        high = picked_high[:].bitcast(BF16).rearrange("p (g h w) -> p g h w", g=G, h=HALVES)
+
         c_codes = [keep.tile([P, P], U32, name="c_codes_%d" % h, align_bytes=64) for h in range(HALVES)]
         c_scales = [keep.tile([P, P], U8, name="c_scales_%d" % h, align_bytes=64) for h in range(HALVES)]
-        for pair in range(2):
-            table = keep.tile([P, 2 * T], BF16, name="table_%d" % pair)
-            start = 0
-            for n, (width, on_vector) in enumerate(CHUNKS[pair]):
-                src = raw[pair, n][:].rearrange("p e t -> p t e")
-                dst = table[:, 2 * start : 2 * (start + width)].rearrange("p (t e) -> p t e", e=2)
-                if on_vector > 0:
-                    nc.vector.tensor_copy(dst[:, :on_vector, :], src[:, :on_vector, :])
-                if on_vector < width:
-                    nc.scalar.copy(dst[:, on_vector:, :], src[:, on_vector:, :])
-                start = start + width
-            picked = keep.tile([P, G * S], U32, name="picked_%d" % pair)
-            nc.vector.tensor_copy(picked[:], table[:].bitcast(U32).indirect(offsets[:]))
-            values = picked[:].bitcast(BF16).rearrange("p (g h w) -> p g h w", g=G, h=HALVES)
-            if pair == 1:
-                for h in range(HALVES):
-                    nc.scalar.copy(
-                        c_grouped[h][:].rearrange("p (a b i) -> p a i b", b=4, i=4),
-                        c_raw[:, :, h * P : (h + 1) * P].rearrange("p i (a b) -> p a i b", b=4),
-                    )
-            if pair == 0:
-                for h in range(HALVES):
-                    nc.vector.tensor_tensor(part[:, pair, h], values[:, 0:2, h, :], values[:, 2:4, h, :], MAX)
+        c_grouped = [keep.tile([P, 4 * P], BF16, name="c_grouped_%d" % h, align_bytes=64) for h in range(HALVES)]
+        for h in range(HALVES):
+            nc.scalar.copy(
+                c_grouped[h][:].rearrange("p (a b i) -> p a i b", b=4, i=4),
+                c_raw[:, :, h * P : (h + 1) * P].rearrange("p i (a b) -> p a i b", b=4),
+            )
+        for h in range(HALVES):
+            nc.vector.quantize_mx(out=c_codes[h][:].bitcast(FP8X4), scales=c_scales[h][:], in_=c_grouped[h][:])
+            nc.vector.tensor_tensor(rows[:, 2 + 2 * h : 4 + 2 * h, :], high[:, 0:2, h, :], high[:, 2:4, h, :], MAX)
 
         x_grouped = [keep.tile([P, 4 * P], BF16, name="x_grouped_%d" % h, align_bytes=64) for h in range(HALVES)]
         x_codes = [keep.tile([P, P], U32, name="x_codes_%d" % h, align_bytes=64) for h in range(HALVES)]
         x_scales = [keep.tile([P, P], U8, name="x_scales_%d" % h, align_bytes=64) for h in range(HALVES)]
-
-        def qc(h):
-            nc.vector.quantize_mx(out=c_codes[h][:].bitcast(FP8X4), scales=c_scales[h][:], in_=c_grouped[h][:])
-
-        def l1(h):
-            nc.vector.tensor_tensor(part[:, 1, h], values[:, 0:2, h, :], values[:, 2:4, h, :], MAX)
-
-        def l2(h):
-            both = part[:, :, h].rearrange("p q u (j e) -> p u j q e", e=2)
+        for h in range(HALVES):
+            both = [
+                rows[:, h : 3 + 2 * h + u : 2 + h + u, :].rearrange("p q (j e) -> p j q e", e=2) for u in range(2)
+            ]
             nc.vector.tensor_tensor(
-                x_grouped[h][:].rearrange("p (j q e) -> p j q e", q=2, e=2), both[:, 0], both[:, 1], MAX
+                x_grouped[h][:].rearrange("p (j q e) -> p j q e", q=2, e=2), both[0], both[1], MAX
             )
-
-        def qx(h):
+        for h in range(HALVES):
             nc.vector.quantize_mx(out=x_codes[h][:].bitcast(FP8X4), scales=x_scales[h][:], in_=x_grouped[h][:])
 
-        qc(0)
-        l1(0)
-        qc(1)
-        l1(1)
-        l2(0)
-        l2(1)
-        qx(0)
-        qx(1)
-
         for h in range(HALVES):
-            for start, width in BANKS:
+            for start, width in BANKS[h]:
                 acc = psum.tile([P, width], F32, name="acc_%d_%d" % (h, start))
                 nc.tensor.matmul_mx(
                     out=acc[:],
                     lhsT=c_codes[h][:].bitcast(FP8X4),
                     lhsT_scale=c_scales[h][:],
                     rhs=w8[:, start : start + width].bitcast(FP8X4),
-                    rhs_scale=w_scales[:, start : start + width],
+                    rhs_scale=w8_plane[:, start : start + width],
                     start=True,
                     stop=False,
                 )
-                step = M if width == M else P
-                for n in range(0, width, step):
+                for n in range(0, width, P):
                     nc.tensor.matmul_mx(
-                        out=acc[:, n : n + step],
+                        out=acc[:, n : n + P],
                         lhsT=x_codes[h][:].bitcast(FP8X4),
                         lhsT_scale=x_scales[h][:],
-                        rhs=w4[:, 2 * (start + n) : 2 * (start + n + step)].bitcast(FP4X4),
-                        rhs_scale=w_scales[:, M + start + n : M + start + n + step],
+                        rhs=w4[:, 2 * (start + n) : 2 * (start + n + P)].bitcast(FP4X4),
+                        rhs_scale=w4_plane[:, start + n : start + n + P],
                         start=False,
-                        stop=(n + step == width),
+                        stop=(n + P == width),
                     )
                 result = keep.tile([P, width], F32, name="result_%d_%d" % (h, start))
                 nc.vector.tensor_tensor(result[:], acc[:], r_sb[:, h, start : start + width], ADD)

from contextlib import ExitStack

import concourse.mybir as mybir

G, K, M, T, S = 4, 512, 512, 2048, 256
FLOPS = 2 * 2 * K * M * S

F32 = mybir.dt.float32
BF16 = mybir.dt.bfloat16
I32 = mybir.dt.int32
U32 = mybir.dt.uint32
U16 = mybir.dt.uint16
U8 = mybir.dt.uint8
FP8X4 = mybir.dt.float8_e4m3fn_x4
FP4X4 = mybir.dt.float4_e2m1fn_x4
MAX = mybir.AluOpType.max
ADD = mybir.AluOpType.add

P = 128
HALVES = S // P
CHUNKS = ((768, 0), (768, 256), (512, 352))
BANKS = (((0, 256), (256, 256)), ((0, 256), (256, 256)))


def load_scale_rows(nc, plane, scales):
    for q in range(4):
        nc.sync.dma_start(plane[32 * q : 32 * q + 4, :].bitcast(I32), scales[0, 4 * q : 4 * q + 4, :].bitcast(I32))


def tile_list_sage_tm_res_kernel(tc, xT, c, w4_words, w4_scales, w8_words, w8_scales, r, offs, out):
    nc = tc.nc
    with ExitStack() as ctx:
        keep = ctx.enter_context(tc.tile_pool(name="keep", bufs=1))
        psum = ctx.enter_context(tc.psum_pool(name="psum", bufs=1))

        offsets = keep.tile([P, G * S // 16], U16, name="offsets")
        x_rows = xT.rearrange("(p i) t -> p i t", i=4)
        plane = [keep.tile([P, T], F32, name="plane_%d" % i) for i in range(2)]
        nc.sync.dma_start(plane[0][:], x_rows[:, 0, :])
        nc.sync.dma_start(offsets[:], offs)
        nc.sync.dma_start(plane[1][:], x_rows[:, 1, :])
        raw = []
        start = 0
        for n, (width, on_vector) in enumerate(CHUNKS):
            raw.append(keep.tile([P, 2, width], F32, name="raw_%d" % n))
            nc.sync.dma_start(raw[n][:], x_rows[:, 2:4, start : start + width])
            start = start + width

        stage = keep.tile([P, S + 4 * S], F32, name="stage")
        c_raw = stage[:, S:].rearrange("p (i j) -> p i j", i=4)
        rows = stage[:, : 3 * S].bitcast(BF16).rearrange("p (n w) -> p n w", w=2 * P)
        nc.sync.dma_start(c_raw, c.rearrange("(p i) j -> p i j", i=4))
        w8 = keep.tile([P, M], U32, name="w8", align_bytes=64)
        nc.sync.dma_start(w8[:].bitcast(I32), w8_words[0].rearrange("p n t -> p (n t)").bitcast(I32))
        w4 = keep.tile([P, 2 * M], U8, name="w4", align_bytes=64)
        nc.sync.dma_start(w4[:].bitcast(I32), w4_words[0].bitcast(I32))
        w8_plane = keep.tile([P, M], U8, name="w8_plane", align_bytes=64)
        load_scale_rows(nc, w8_plane, w8_scales)
        r_sb = keep.tile([P, HALVES, M], F32, name="r_sb")
        nc.sync.dma_start(r_sb[:], r.rearrange("(h p) n -> p h n", p=P))
        w4_plane = keep.tile([P, M], U8, name="w4_plane", align_bytes=64)
        load_scale_rows(nc, w4_plane, w4_scales)

        picked_low = keep.tile([P, 2, G * S], BF16, name="picked_low")
        for i in range(2):
            nc.vector.tensor_copy(picked_low[:, i, :], plane[i][:].indirect(offsets[:]))
        low = keep.tile([P, 2, 2 * S], BF16, name="low")
        nc.vector.tensor_tensor(low[:], picked_low[:, :, : 2 * S], picked_low[:, :, 2 * S :], MAX)
        low_u = low[:].rearrange("p e (u h j) -> p u h j e", u=2, h=HALVES)
        for h in range(HALVES):
            nc.vector.tensor_tensor(rows[:, h, :].rearrange("p (j e) -> p j e", e=2), low_u[:, 0, h], low_u[:, 1, h], MAX)

        table = keep.tile([P, 2 * T], BF16, name="table")
        start = 0
        for n, (width, on_vector) in enumerate(CHUNKS):
            src = raw[n][:].rearrange("p e t -> p t e")
            dst = table[:, 2 * start : 2 * (start + width)].rearrange("p (t e) -> p t e", e=2)
            if on_vector > 0:
                nc.vector.tensor_copy(dst[:, :on_vector, :], src[:, :on_vector, :])
            if on_vector < width:
                nc.scalar.copy(dst[:, on_vector:, :], src[:, on_vector:, :])
            start = start + width
        picked_high = keep.tile([P, G * S], U32, name="picked_high")
        nc.vector.tensor_copy(picked_high[:], table[:].bitcast(U32).indirect(offsets[:]))
        high = picked_high[:].bitcast(BF16).rearrange("p (g h w) -> p g h w", g=G, h=HALVES)

        c_codes = [keep.tile([P, P], U32, name="c_codes_%d" % h, align_bytes=64) for h in range(HALVES)]
        c_scales = [keep.tile([P, P], U8, name="c_scales_%d" % h, align_bytes=64) for h in range(HALVES)]
        c_grouped = [keep.tile([P, 4 * P], BF16, name="c_grouped_%d" % h, align_bytes=64) for h in range(HALVES)]
        for h in range(HALVES):
            nc.scalar.copy(
                c_grouped[h][:].rearrange("p (a b i) -> p a i b", b=4, i=4),
                c_raw[:, :, h * P : (h + 1) * P].rearrange("p i (a b) -> p a i b", b=4),
            )
        for h in range(HALVES):
            nc.vector.quantize_mx(out=c_codes[h][:].bitcast(FP8X4), scales=c_scales[h][:], in_=c_grouped[h][:])
            nc.vector.tensor_tensor(rows[:, 2 + 2 * h : 4 + 2 * h, :], high[:, 0:2, h, :], high[:, 2:4, h, :], MAX)

        x_grouped = [keep.tile([P, 4 * P], BF16, name="x_grouped_%d" % h, align_bytes=64) for h in range(HALVES)]
        x_codes = [keep.tile([P, P], U32, name="x_codes_%d" % h, align_bytes=64) for h in range(HALVES)]
        x_scales = [keep.tile([P, P], U8, name="x_scales_%d" % h, align_bytes=64) for h in range(HALVES)]
        for h in range(HALVES):
            both = [
                rows[:, h : 3 + 2 * h + u : 2 + h + u, :].rearrange("p q (j e) -> p j q e", e=2) for u in range(2)
            ]
            nc.vector.tensor_tensor(
                x_grouped[h][:].rearrange("p (j q e) -> p j q e", q=2, e=2), both[0], both[1], MAX
            )
        for h in range(HALVES):
            nc.vector.quantize_mx(out=x_codes[h][:].bitcast(FP8X4), scales=x_scales[h][:], in_=x_grouped[h][:])

        for h in range(HALVES):
            for start, width in BANKS[h]:
                acc = psum.tile([P, width], F32, name="acc_%d_%d" % (h, start))
                nc.tensor.matmul_mx(
                    out=acc[:],
                    lhsT=c_codes[h][:].bitcast(FP8X4),
                    lhsT_scale=c_scales[h][:],
                    rhs=w8[:, start : start + width].bitcast(FP8X4),
                    rhs_scale=w8_plane[:, start : start + width],
                    start=True,
                    stop=False,
                )
                for n in range(0, width, P):
                    nc.tensor.matmul_mx(
                        out=acc[:, n : n + P],
                        lhsT=x_codes[h][:].bitcast(FP8X4),
                        lhsT_scale=x_scales[h][:],
                        rhs=w4[:, 2 * (start + n) : 2 * (start + n + P)].bitcast(FP4X4),
                        rhs_scale=w4_plane[:, start + n : start + n + P],
                        start=False,
                        stop=(n + P == width),
                    )
                result = keep.tile([P, width], F32, name="result_%d_%d" % (h, start))
                nc.vector.tensor_tensor(result[:], acc[:], r_sb[:, h, start : start + width], ADD)
                nc.sync.dma_start(out[h * P : (h + 1) * P, start : start + width], result[:])
